import numpy as np
import ml_dtypes


def mxq(x, axis, fmt="e4m3"):
    dtype, down = {"e4m3": (ml_dtypes.float8_e4m3fn, 7), "e5m2": (ml_dtypes.float8_e5m2, 14)}[fmt]
    v = np.moveaxis(np.asarray(x, np.float32).astype(ml_dtypes.bfloat16).astype(np.float64), axis, -1)
    blocks = v.reshape(v.shape[:-1] + (-1, 32))
    amax = np.abs(blocks).max(-1, keepdims=True)
    byte = np.maximum(np.where(amax > 0, np.frexp(amax)[1] - 1 + 127, 0) - down, 1)
    scale = np.exp2(byte - 127.0)
    codes = (blocks / scale).astype(np.float32).astype(dtype).astype(np.float64)
    return np.moveaxis((codes * scale).reshape(v.shape), -1, axis)


WIDE = False


def mx_kscale(k):
    if not WIDE:
        return np.ones(k)
    levels = np.array([10, -10, 5, -5, 0])
    if k % 512:
        return np.exp2(np.random.permutation(np.resize(levels, k // 32))).repeat(32)
    a = np.empty((k // 512, 16))
    for p in range(k // 512):
        a[p, :8] = np.random.permutation(np.resize(levels, 8))
        for g in range(8):
            far = levels[np.abs(levels - a[p, g]) >= 10]
            a[p, g + 8] = far[np.random.randint(len(far))]
    return np.exp2(a.ravel()).repeat(32)


def f64(x):
    return np.asarray(x).astype(np.float64)


def striped(idx):
    return np.tile(np.asarray(idx).reshape(-1, 16).T, (8, 1)).astype(np.uint16)


def unstriped(offs):
    return offs[:16].T.reshape(-1).astype(np.int64)


def striped8(idx):
    return np.asarray(idx).reshape(8, -1, 16).transpose(0, 2, 1).reshape(128, -1).astype(np.uint16)


def unstriped8(offs):
    return offs.reshape(8, 16, -1).transpose(0, 2, 1).reshape(8, -1).astype(np.int64)


def pick8(x, idx, run):
    r = np.arange(len(x))
    return x[r[:, None], idx[r % (8 * run) // run]]


E2M1 = np.array([0.0, 0.5, 1.0, 1.5, 2.0, 3.0, 4.0, 6.0, -0.0, -0.5, -1.0, -1.5, -2.0, -3.0, -4.0, -6.0])


def pack_weight(w, fmt):
    k, n = w.shape
    w = f64(np.asarray(w, np.float32).astype(ml_dtypes.bfloat16)).reshape(k // 32, 32, n)
    amax = np.abs(w).max(1)
    if fmt == "e4m3":
        byte = np.frexp(amax)[1] - 1 + 127 - 7
    else:
        mant, ex = np.frexp(amax / 6.0)
        byte = np.where(mant > 0.5, ex, ex - 1) + 127
    byte = np.clip(np.where(amax > 0, byte, 1), 1, 254)
    scaled = (w * np.exp2(127.0 - byte)[:, None, :]).reshape(k, n).astype(np.float32)
    by_word = np.ascontiguousarray(scaled.reshape(k // 512, 128, 4, n).transpose(0, 1, 3, 2))
    if fmt == "e4m3":
        words = by_word.astype(ml_dtypes.float8_e4m3fn).view(np.uint8)
    else:
        c = by_word.astype(ml_dtypes.float4_e2m1fn).view(np.uint8) & 0xF
        words = (c[..., 0::2] | (c[..., 1::2] << 4)).reshape(k // 512, 128, 2 * n)
    return np.ascontiguousarray(words), np.ascontiguousarray(byte.astype(np.uint8).reshape(k // 512, 16, n))


def unpack_weight(words, scales, fmt):
    g, _, n = scales.shape
    words = np.ascontiguousarray(words).reshape(g, 128, n, -1)
    if fmt == "e4m3":
        vals = words.view(ml_dtypes.float8_e4m3fn).astype(np.float64)
    else:
        nib = np.empty((g, 128, n, 4), np.uint8)
        nib[..., 0::2] = words & 0xF
        nib[..., 1::2] = words >> 4
        vals = E2M1[nib]
    vals = vals * np.repeat(np.exp2(scales.astype(np.float64) - 127.0), 8, axis=1)[..., None]
    return vals.transpose(0, 1, 3, 2).reshape(g * 512, n)


K, J, R, T, F, G, O, S, N = 512, 1024, 512, 2048, 1024, 1024, 256, 512, 256


def setup_inputs():
    n = np.random.standard_normal
    idx = np.random.permutation(T)[:J]
    idx2 = np.stack([np.random.permutation(F)[:R] for _ in range(8)])
    idx3 = np.stack([np.random.permutation(G)[:R] for _ in range(8)])
    idx4 = np.stack([np.random.permutation(J)[:S] for _ in range(8)])
    idx5 = np.stack([np.random.permutation(S)[:O] for _ in range(8)])
    idx6 = np.random.permutation(S)[:O]
    idx7 = np.random.permutation(T)[:O]
    fk = mx_kscale(K)
    fr = mx_kscale(R)
    xtp = pack_weight(n((K, T)) * fk[:, None], "e4m3")
    wbp = pack_weight(n((R, N)) * 1 / np.sqrt(R) / fr[:, None], "e2m1")
    wsp = pack_weight(n((K, N)) * 1 / np.sqrt(K) / fk[:, None], "e2m1")
    return {
        "xt_words": xtp[0],
        "xt_scales": xtp[1],
        "ua": (np.random.randint(-7, 8, (K, F)).astype(np.float64)).astype(np.float32),
        "ub": (np.random.randint(-7, 8, (K, G)).astype(np.float64)).astype(np.float32),
        "ha": ((np.random.randint(8, 25, (K, 1)) / 1024.0) / fk[:, None]).astype(np.float32),
        "hb": ((np.random.randint(8, 25, (K, 1)) / 1024.0) / fk[:, None]).astype(np.float32),
        "sa": (np.random.uniform(0.5, 1.6, (R, 1)) * fr[:, None]).astype(np.float32),
        "sb": (np.random.uniform(0.5, 1.6, (R, 1))).astype(np.float32),
        "sd": (np.random.uniform(0.5, 1.6, (R, 1))).astype(np.float32),
        "wb_words": wbp[0],
        "wb_scales": wbp[1],
        "ws_words": wsp[0],
        "ws_scales": wsp[1],
        "offs": striped(idx),
        "offs2": striped8(idx2),
        "offs3": striped8(idx3),
        "offs4": striped8(idx4),
        "offs5": striped8(idx5),
        "offs6": striped(idx6),
        "offs7": striped(idx7),
    }


def reference(xt_words, xt_scales, ua, ub, ha, hb, sa, sb, sd, wb_words, wb_scales, ws_words, ws_scales, offs, offs2, offs3, offs4, offs5, offs6, offs7):
    idx = unstriped(offs)
    idx2 = unstriped8(offs2)
    idx3 = unstriped8(offs3)
    idx4 = unstriped8(offs4)
    idx5 = unstriped8(offs5)
    idx6 = unstriped(offs6)
    idx7 = unstriped(offs7)
    xtu = unpack_weight(xt_words, xt_scales, "e4m3")
    wbu = unpack_weight(wb_words, wb_scales, "e2m1")
    wsu = unpack_weight(ws_words, ws_scales, "e2m1")
    wc = np.maximum(pick8(f64(ua), idx2, 64) * f64(ha), pick8(f64(ub), idx3, 64) * f64(hb))
    wcq = mxq(wc, 0, "e4m3")
    xtidxg = xtu[:, idx]
    a = wcq.T @ xtidxg
    h1 = pick8(a, idx4, 64) * f64(sa)
    hid = np.maximum(pick8(h1, idx5, 64) * f64(sb), h1[:, idx6] * f64(sd))
    hidq = mxq(hid, 0, "e4m3")
    xtidx7g = xtu[:, idx7]
    y = wbu.T @ hidq + wsu.T @ xtidx7g
    return y

@@ -1,0 +1,258 @@
+from contextlib import ExitStack
+
+import concourse.mybir as mybir
+
+K, J, R, T, F, O, S, N = 512, 1024, 512, 2048, 1024, 256, 512, 256
+FLOPS = 2 * K * R * J + 2 * R * N * O + 2 * K * N * O
+
+F32 = mybir.dt.float32
+BF16 = mybir.dt.bfloat16
+I32 = mybir.dt.int32
+U32 = mybir.dt.uint32
+U16 = mybir.dt.uint16
+U8 = mybir.dt.uint8
+FP8X4 = mybir.dt.float8_e4m3fn_x4
+FP4X4 = mybir.dt.float4_e2m1fn_x4
+COPY = mybir.ActivationFunctionType.Copy
+MAX = mybir.AluOpType.max
+
+P = 128
+PACK = 4
+LAST = PACK - 1
+LANES = 16
+BANK = 512
+QUADRANTS = 4
+
+
+def tile_picked_tokens_largercode_one_chain_further_plain_kernel(
+    tc, xt_words, xt_scales, ua, ub, ha, hb, sa, sb, sd, wb_words, wb_scales, ws_words, ws_scales,
+    offs, offs2, offs3, offs4, offs5, offs6, offs7, out,
+):
+    nc = tc.nc
+    with ExitStack() as ctx:
+        lists = ctx.enter_context(tc.tile_pool(name="lists", bufs=1))
+        keep = ctx.enter_context(tc.tile_pool(name="keep", bufs=1))
+        psum = ctx.enter_context(tc.psum_pool(name="psum", bufs=1))
+
+        def load_list(name, source):
+            tile = lists.tile(list(source.shape), U16, name=name)
+            nc.sync.dma_start(tile[:], source)
+            return tile
+
+        def load_factors(name, source, queue):
+            tile = keep.tile([P, PACK], F32, name=name)
+            queue.dma_start(tile[:], source.rearrange("(p t) o -> p (t o)", t=PACK))
+            return tile
+
+        def load_rows(name, source, t):
+            tile = keep.tile([P, F], F32, name=name)
+            nc.sync.dma_start(tile[:], source.rearrange("(p t) f -> p t f", t=PACK)[:, t, :])
+            return tile
+
+        def cleared_plane(name, width):
+            tile = keep.tile([P, width], U8, name=name, align_bytes=64)
+            nc.vector.memset(tile[:].bitcast(I32), 0)
+            return tile
+
+        def load_scale_rows(tile, source, q):
+            nc.sync.dma_start(
+                tile[32 * q : 32 * q + 4, :].bitcast(I32),
+                source[0, 4 * q : 4 * q + 4, :].bitcast(I32),
+            )
+
+        def load_fp4_words(name, source):
+            tile = keep.tile([P, 2 * N], U8, name=name, align_bytes=64)
+            nc.sync.dma_start(tile[:].bitcast(I32), source[0].bitcast(I32))
+            return tile
+
+        def fetch(dst, window, offsets, first, count, factor):
+            cols = slice(first // LANES, (first + count) // LANES)
+            nc.scalar.activation(
+                out=dst[:, first : first + count],
+                in_=window[:].indirect(offsets[:, cols]),
+                func=COPY,
+                scale=factor,
+            )
+
+        def gather_packed(dst, window, offsets, first, count):
+            cols = slice(first // LANES, (first + count) // LANES)
+            nc.vector.tensor_copy(out=dst[:, first : first + count], in_=window[:].indirect(offsets[:, cols]))
+
+        def quantize(codes, scales, grouped, first, count):
+            nc.vector.quantize_mx(
+                out=codes[:, first : first + count].bitcast(FP8X4),
+                scales=scales[:, first : first + count],
+                in_=grouped[:, first : first + count, :].rearrange("p c t -> p (c t)"),
+            )
+
+        x_scale_rows = cleared_plane("x_scale_rows", T)
+        ws_scale_rows = cleared_plane("ws_scale_rows", N)
+        wb_scale_rows = cleared_plane("wb_scale_rows", N)
+        ha_t = load_factors("ha_t", ha, nc.scalar)
+        hb_t = load_factors("hb_t", hb, nc.scalar)
+        ua_rows, ub_rows = [], []
+        list2 = load_list("list2", offs2)
+        ua_rows.append(load_rows("ua0", ua, 0))
+        list3 = load_list("list3", offs3)
+        ub_rows.append(load_rows("ub0", ub, 0))
+        ua_rows.append(load_rows("ua1", ua, 1))
+        list1 = load_list("list1", offs)
+        for q in range(QUADRANTS):
+            load_scale_rows(x_scale_rows, xt_scales, q)
+        ub_rows.append(load_rows("ub1", ub, 1))
+        ua_rows.append(load_rows("ua2", ua, 2))
+        x_words = keep.tile([P, T], U32, name="x_words")
+        nc.sync.dma_start(x_words[:].bitcast(I32), xt_words[0].rearrange("p c t -> p (c t)").bitcast(I32))
+        ub_rows.append(load_rows("ub2", ub, 2))
+        ua_rows.append(load_rows("ua3", ua, 3))
+        ub_rows.append(load_rows("ub3", ub, 3))
+        list4 = load_list("list4", offs4)
+        sa_t = load_factors("sa_t", sa, nc.sync)
+        list5 = load_list("list5", offs5)
+        sb_t = load_factors("sb_t", sb, nc.sync)
+        list6 = load_list("list6", offs6)
+        sd_t = load_factors("sd_t", sd, nc.sync)
+        list7 = load_list("list7", offs7)
+        ws_codes = load_fp4_words("ws_codes", ws_words)
+        wb_codes = load_fp4_words("wb_codes", wb_words)
+        for q in range(QUADRANTS):
+            load_scale_rows(ws_scale_rows, ws_scales, q)
+        for q in range(QUADRANTS):
+            load_scale_rows(wb_scale_rows, wb_scales, q)
+
+        slot_codes = keep.tile([P, J], U32, name="slot_codes", align_bytes=64)
+        slot_scales = keep.tile([P, J], U8, name="slot_scales", align_bytes=64)
+        first_prod = [keep.tile([P, R], F32, name="first_prod%d" % t) for t in range(PACK)]
+        second_prod = [keep.tile([P, R], F32, name="second_prod%d" % t, tag="second_prod%d" % t, align_bytes=64) for t in range(PACK)]
+        wc_early = keep.tile([P, LAST, R], BF16, name="wc_early")
+        wc_grouped = [keep.tile([P, P, PACK], BF16, name="wc_grouped%d" % u, tag="wc_grouped%d" % u, align_bytes=64) for u in range(PACK)]
+        wc_codes = [keep.tile([P, P], U32, name="wc_codes%d" % u, align_bytes=64) for u in range(PACK)]
+        wc_scales = [keep.tile([P, P], U8, name="wc_scales%d" % u, align_bytes=64) for u in range(PACK)]
+
+        for t in range(LAST):
+            fetch(first_prod[t], ua_rows[t], list2, 0, R, ha_t[:, t : t + 1])
+            fetch(second_prod[t], ub_rows[t], list3, 0, R, hb_t[:, t : t + 1])
+            if t == 1:
+                gather_packed(slot_scales, x_scale_rows, list1, 0, J)
+            if t == LAST - 1:
+                for first in range(0, J, BANK):
+                    gather_packed(slot_codes, x_words, list1, first, BANK)
+            nc.vector.tensor_tensor(out=wc_early[:, t, :], in0=first_prod[t][:], in1=second_prod[t][:], op=MAX)
+
+        def group_early_wc(u):
+            nc.vector.tensor_copy(
+                out=wc_grouped[u][:, :, 0:LAST],
+                in_=wc_early[:].rearrange("p t (m u) -> p u m t", u=PACK)[:, u, :, :],
+            )
+
+        def finish_wc(u, first, count):
+            cols = slice(first, first + count)
+            nc.vector.tensor_tensor(
+                out=wc_grouped[u][:, cols, LAST],
+                in0=first_prod[LAST][:].rearrange("p (m u) -> p u m", u=PACK)[:, u, cols],
+                in1=second_prod[LAST][:].rearrange("p (m u) -> p u m", u=PACK)[:, u, cols],
+                op=MAX,
+            )
+            quantize(wc_codes[u], wc_scales[u], wc_grouped[u], first, count)
+
+        for u in range(PACK):
+            group_early_wc(u)
+        fetch(first_prod[LAST], ua_rows[LAST], list2, 0, R, ha_t[:, LAST:PACK])
+        for half in range(2):
+            fetch(second_prod[LAST], ub_rows[LAST], list3, half * R // 2, R // 2, hb_t[:, LAST:PACK])
+            finish_wc(0, half * P // 2, P // 2)
+
+        a_rows = [keep.tile([P, J], F32, name="a_rows%d" % u) for u in range(PACK)]
+        seats = [keep.tile([P, S], F32, name="seats%d" % u) for u in range(PACK)]
+        by_group = [keep.tile([P, O], F32, name="by_group%d" % u) for u in range(PACK)]
+        by_all = [keep.tile([P, O], F32, name="by_all%d" % u) for u in range(PACK)]
+        hid_grouped = keep.tile([P, O, PACK], BF16, name="hid_grouped", align_bytes=64)
+        hid_codes = keep.tile([P, O], U32, name="hid_codes", align_bytes=64)
+        hid_scales = keep.tile([P, O], U8, name="hid_scales", align_bytes=64)
+
+        def first_product(u, width, bank_tags):
+            for i, first in enumerate(range(0, J, width)):
+                cols = slice(first, first + width)
+                acc = psum.tile([P, width], F32, name="acc", tag=bank_tags[i])
+                nc.tensor.matmul_mx(
+                    out=acc[:],
+                    lhsT=wc_codes[u][:].bitcast(FP8X4),
+                    lhsT_scale=wc_scales[u][:],
+                    rhs=slot_codes[:, cols].bitcast(FP8X4),
+                    rhs_scale=slot_scales[:, cols],
+                    start=True,
+                    stop=True,
+                )
+                if u == 0:
+                    nc.scalar.copy(out=a_rows[u][:, cols], in_=acc[:])
+                else:
+                    nc.vector.tensor_copy(out=a_rows[u][:, cols], in_=acc[:])
+
+        def fetch_seats(u):
+            fetch(seats[u], a_rows[u], list4, 0, S, sa_t[:, u : u + 1])
+
+        def fetch_by_group(u):
+            fetch(by_group[u], seats[u], list5, 0, O, sb_t[:, u : u + 1])
+
+        def fetch_by_all(u, first, count):
+            fetch(by_all[u], seats[u], list6, first, count, sd_t[:, u : u + 1])
+
+        first_product(0, BANK // 2, ["bank0", "bank1", "bank2", "bank3"])
+        fetch_seats(0)
+        fetch_by_group(0)
+        later_banks = {1: ["bank4", "bank5"], 2: ["bank6", "bank7"], 3: ["bank0", "bank1"]}
+        for u in range(1, PACK):
+            finish_wc(u, 0, P)
+            first_product(u, BANK, later_banks[u])
+            fetch_seats(u)
+            fetch_by_all(u - 1, 0, O)
+            nc.vector.tensor_tensor(out=hid_grouped[:, :, u - 1], in0=by_group[u - 1][:], in1=by_all[u - 1][:], op=MAX)
+            fetch_by_group(u)
+
+        short_codes = keep.tile([P, O], U32, name="short_codes", tag="wc_grouped%d" % LAST, align_bytes=64)
+        short_scales = keep.tile([P, O], U8, name="short_scales", tag="second_prod%d" % LAST, align_bytes=64)
+        gather_packed(short_codes, x_words, list7, 0, O)
+        gather_packed(short_scales, x_scale_rows, list7, 0, O)
+        width = O // 2
+        pieces = [(half, h) for half in range(2) for h in range(N // P)]
+        sums = {}
+        for i, (half, h) in enumerate(pieces):
+            sums[half, h] = psum.tile([P, width], F32, name="sums", tag="bank%d" % (2 + i))
+            cols = slice(half * width, (half + 1) * width)
+            nc.tensor.matmul_mx(
+                out=sums[half, h][:],
+                lhsT=ws_codes[:, 2 * P * h : 2 * P * (h + 1)].bitcast(FP4X4),
+                lhsT_scale=ws_scale_rows[:, P * h : P * (h + 1)],
+                rhs=short_codes[:, cols].bitcast(FP8X4),
+                rhs_scale=short_scales[:, cols],
+                start=True,
+                stop=False,
+            )
+
+        for half in range(2):
+            cols = slice(half * width, (half + 1) * width)
+            fetch_by_all(LAST, half * width, width)
+            nc.vector.tensor_tensor(
+                out=hid_grouped[:, cols, LAST], in0=by_group[LAST][:, cols], in1=by_all[LAST][:, cols], op=MAX
+            )
+        for half in range(2):
+            quantize(hid_codes, hid_scales, hid_grouped, half * width, width)
+
+        for half, h in pieces:
+            cols = slice(half * width, (half + 1) * width)
+            nc.tensor.matmul_mx(
+                out=sums[half, h][:],
+                lhsT=wb_codes[:, 2 * P * h : 2 * P * (h + 1)].bitcast(FP4X4),
+                lhsT_scale=wb_scale_rows[:, P * h : P * (h + 1)],
+                rhs=hid_codes[:, cols].bitcast(FP8X4),
+                rhs_scale=hid_scales[:, cols],
+                start=False,
+                stop=True,
+            )
+            result = keep.tile([P, width], F32, name="result%d%d" % (half, h))
+            if h == 0:
+                nc.vector.tensor_copy(out=result[:], in_=sums[half, h][:])
+                nc.sync.dma_start(out[P * h : P * (h + 1), cols], result[:])
+            else:
+                nc.scalar.copy(out=result[:], in_=sums[half, h][:])
+                nc.scalar.dma_start(out[P * h : P * (h + 1), cols], result[:])

@@ -94,11 +94,21 @@ def tile_picked_tokens_largercode_one_chain_further_plain_kernel(
         list2 = load_list("list2", offs2)
         ua_rows.append(load_rows("ua0", ua, 0))
         list3 = load_list("list3", offs3)
-        ub_rows.append(load_rows("ub0", ub, 0))
-        ua_rows.append(load_rows("ua1", ua, 1))
-        list1 = load_list("list1", offs)
+        x_scale_staged = keep.tile([P, 2, T], U8, name="x_scale_staged")
+        for half in range(2):
+            nc.sync.dma_start(
+                x_scale_staged[64 * half : 64 * half + 4, :, :].bitcast(I32),
+                xt_scales[0, 8 * half : 8 * half + 8, :].rearrange("(q r) c -> r q c", q=2).bitcast(I32),
+            )
         for q in range(QUADRANTS):
-            load_scale_rows(x_scale_rows, xt_scales, q)
+            source = 64 * (q // 2)
+            nc.vector.tensor_copy(
+                out=x_scale_rows[32 * q : 32 * q + 4, :].bitcast(I32),
+                in_=x_scale_staged[source : source + 4, q % 2, :].bitcast(I32),
+            )
+        ub_rows.append(load_rows("ub0", ub, 0))
+        list1 = load_list("list1", offs)
+        ua_rows.append(load_rows("ua1", ua, 1))
         ub_rows.append(load_rows("ub1", ub, 1))
         ua_rows.append(load_rows("ua2", ua, 2))
         x_words = keep.tile([P, T], U32, name="x_words")
@@ -120,64 +130,69 @@ def tile_picked_tokens_largercode_one_chain_further_plain_kernel(
         for q in range(QUADRANTS):
             load_scale_rows(wb_scale_rows, wb_scales, q)
 
-        slot_codes = keep.tile([P, J], U32, name="slot_codes", align_bytes=64)
-        slot_scales = keep.tile([P, J], U8, name="slot_scales", align_bytes=64)
+        slot_codes = keep.tile([P, J], U32, name="slot_codes", tag="slot_codes", align_bytes=64)
+        slot_scales = keep.tile([P, J], U8, name="slot_scales", tag="slot_scales", align_bytes=64)
         first_prod = [keep.tile([P, R], F32, name="first_prod%d" % t) for t in range(PACK)]
-        second_prod = [keep.tile([P, R], F32, name="second_prod%d" % t, tag="second_prod%d" % t, align_bytes=64) for t in range(PACK)]
-        wc_early = keep.tile([P, LAST, R], BF16, name="wc_early")
-        wc_grouped = [keep.tile([P, P, PACK], BF16, name="wc_grouped%d" % u, tag="wc_grouped%d" % u, align_bytes=64) for u in range(PACK)]
-        wc_codes = [keep.tile([P, P], U32, name="wc_codes%d" % u, align_bytes=64) for u in range(PACK)]
-        wc_scales = [keep.tile([P, P], U8, name="wc_scales%d" % u, align_bytes=64) for u in range(PACK)]
+        second_prod = [keep.tile([P, R], F32, name="second_prod%d" % t) for t in range(LAST)]
+        second_last = [keep.tile([P, R // 2], F32, name="second_last%d" % half) for half in range(2)]
+        wc_plain = keep.tile([P, PACK, R], BF16, name="wc_plain")
+        wc_first = keep.tile([P, P, PACK], BF16, name="wc_first", align_bytes=64)
 
+        gather_packed(slot_scales, x_scale_rows, list1, 0, J)
         for t in range(LAST):
             fetch(first_prod[t], ua_rows[t], list2, 0, R, ha_t[:, t : t + 1])
             fetch(second_prod[t], ub_rows[t], list3, 0, R, hb_t[:, t : t + 1])
-            if t == 1:
-                gather_packed(slot_scales, x_scale_rows, list1, 0, J)
             if t == LAST - 1:
                 for first in range(0, J, BANK):
                     gather_packed(slot_codes, x_words, list1, first, BANK)
-            nc.vector.tensor_tensor(out=wc_early[:, t, :], in0=first_prod[t][:], in1=second_prod[t][:], op=MAX)
+            nc.vector.tensor_tensor(out=wc_plain[:, t, :], in0=first_prod[t][:], in1=second_prod[t][:], op=MAX)
 
-        def group_early_wc(u):
-            nc.vector.tensor_copy(
-                out=wc_grouped[u][:, :, 0:LAST],
-                in_=wc_early[:].rearrange("p t (m u) -> p u m t", u=PACK)[:, u, :, :],
-            )
-
-        def finish_wc(u, first, count):
-            cols = slice(first, first + count)
-            nc.vector.tensor_tensor(
-                out=wc_grouped[u][:, cols, LAST],
-                in0=first_prod[LAST][:].rearrange("p (m u) -> p u m", u=PACK)[:, u, cols],
-                in1=second_prod[LAST][:].rearrange("p (m u) -> p u m", u=PACK)[:, u, cols],
-                op=MAX,
-            )
-            quantize(wc_codes[u], wc_scales[u], wc_grouped[u], first, count)
-
-        for u in range(PACK):
-            group_early_wc(u)
+        dealt = wc_plain[:].rearrange("p t (m u) -> p u m t", u=PACK)
+        nc.vector.tensor_copy(out=wc_first[:, :, 0:LAST], in_=dealt[:, 0, :, 0:LAST])
         fetch(first_prod[LAST], ua_rows[LAST], list2, 0, R, ha_t[:, LAST:PACK])
         for half in range(2):
-            fetch(second_prod[LAST], ub_rows[LAST], list3, half * R // 2, R // 2, hb_t[:, LAST:PACK])
-            finish_wc(0, half * P // 2, P // 2)
+            entries = slice(half * R // 2, (half + 1) * R // 2)
+            nc.scalar.activation(
+                out=second_last[half][:],
+                in_=ub_rows[LAST][:].indirect(list3[:, entries.start // LANES : entries.stop // LANES]),
+                func=COPY,
+                scale=hb_t[:, LAST:PACK],
+            )
+            left = first_prod[LAST][:, entries].rearrange("p (m u) -> p m u", u=PACK)
+            right = second_last[half][:].rearrange("p (m u) -> p m u", u=PACK)
+            nc.vector.tensor_tensor(
+                out=wc_first[:, half * P // 2 : (half + 1) * P // 2, LAST], in0=left[:, :, 0], in1=right[:, :, 0], op=MAX
+            )
+            nc.vector.tensor_tensor(
+                out=wc_plain[:, LAST, entries].rearrange("p (m u) -> p m u", u=PACK)[:, :, 1:PACK],
+                in0=left[:, :, 1:PACK],
+                in1=right[:, :, 1:PACK],
+                op=MAX,
+            )
 
         a_rows = [keep.tile([P, J], F32, name="a_rows%d" % u) for u in range(PACK)]
-        seats = [keep.tile([P, S], F32, name="seats%d" % u) for u in range(PACK)]
-        by_group = [keep.tile([P, O], F32, name="by_group%d" % u) for u in range(PACK)]
-        by_all = [keep.tile([P, O], F32, name="by_all%d" % u) for u in range(PACK)]
-        hid_grouped = keep.tile([P, O, PACK], BF16, name="hid_grouped", align_bytes=64)
+        seats = [keep.tile([P, S], F32, name="seats%d" % u, tag="seats%d" % u, align_bytes=64) for u in range(PACK)]
+        by_group, by_all = [], []
         hid_codes = keep.tile([P, O], U32, name="hid_codes", align_bytes=64)
         hid_scales = keep.tile([P, O], U8, name="hid_scales", align_bytes=64)
 
-        def first_product(u, width, bank_tags):
-            for i, first in enumerate(range(0, J, width)):
+        def first_product(u, widths, banks):
+            if u == 0:
+                grouped = wc_first
+            else:
+                grouped = keep.tile([P, P, PACK], BF16, name="grouped%d" % u, align_bytes=64)
+                nc.vector.tensor_copy(out=grouped[:], in_=dealt[:, u, :, :])
+            wc_codes = keep.tile([P, P], U32, name="wc_codes%d" % u, tag="wc_codes%d" % u, align_bytes=64)
+            wc_scales = keep.tile([P, P], U8, name="wc_scales%d" % u, tag="wc_scales%d" % u, align_bytes=64)
+            quantize(wc_codes, wc_scales, grouped, 0, P)
+            first = 0
+            for width, bank in zip(widths, banks):
                 cols = slice(first, first + width)
-                acc = psum.tile([P, width], F32, name="acc", tag=bank_tags[i])
+                acc = psum.tile([P, width], F32, name="acc", tag="bank%d" % bank)
                 nc.tensor.matmul_mx(
                     out=acc[:],
-                    lhsT=wc_codes[u][:].bitcast(FP8X4),
-                    lhsT_scale=wc_scales[u][:],
+                    lhsT=wc_codes[:].bitcast(FP8X4),
+                    lhsT_scale=wc_scales[:],
                     rhs=slot_codes[:, cols].bitcast(FP8X4),
                     rhs_scale=slot_scales[:, cols],
                     start=True,
@@ -187,32 +202,47 @@ def tile_picked_tokens_largercode_one_chain_further_plain_kernel(
                     nc.scalar.copy(out=a_rows[u][:, cols], in_=acc[:])
                 else:
                     nc.vector.tensor_copy(out=a_rows[u][:, cols], in_=acc[:])
+                first += width
 
         def fetch_seats(u):
             fetch(seats[u], a_rows[u], list4, 0, S, sa_t[:, u : u + 1])
 
         def fetch_by_group(u):
+            by_group.append(keep.tile([P, O], F32, name="by_group", tag="wc_codes%d" % (2 + u % 2), align_bytes=64))
+            by_all.append(keep.tile([P, O], F32, name="by_all", tag="wc_scales%d" % (2 + u % 2), align_bytes=64))
             fetch(by_group[u], seats[u], list5, 0, O, sb_t[:, u : u + 1])
 
         def fetch_by_all(u, first, count):
             fetch(by_all[u], seats[u], list6, first, count, sd_t[:, u : u + 1])
 
-        first_product(0, BANK // 2, ["bank0", "bank1", "bank2", "bank3"])
+        first_product(0, [256, 256, 256, 256], [0, 1, 2, 3])
         fetch_seats(0)
-        fetch_by_group(0)
-        later_banks = {1: ["bank4", "bank5"], 2: ["bank6", "bank7"], 3: ["bank0", "bank1"]}
-        for u in range(1, PACK):
-            finish_wc(u, 0, P)
-            first_product(u, BANK, later_banks[u])
-            fetch_seats(u)
-            fetch_by_all(u - 1, 0, O)
-            nc.vector.tensor_tensor(out=hid_grouped[:, :, u - 1], in0=by_group[u - 1][:], in1=by_all[u - 1][:], op=MAX)
-            fetch_by_group(u)
+        first_product(1, [256, 256, 256, 256], [4, 5, 6, 7])
+        fetch_seats(1)
+        first_product(2, [BANK, BANK], [0, 7])
+        first_product(3, [BANK, BANK], [1, 7])
 
-        short_codes = keep.tile([P, O], U32, name="short_codes", tag="wc_grouped%d" % LAST, align_bytes=64)
-        short_scales = keep.tile([P, O], U8, name="short_scales", tag="second_prod%d" % LAST, align_bytes=64)
+        def larger(u, cols):
+            nc.vector.tensor_tensor(out=hid_grouped[:, cols, u], in0=by_group[u][:, cols], in1=by_all[u][:, cols], op=MAX)
+
+        fetch_by_group(0)
+        fetch_by_all(0, 0, O)
+        fetch_seats(2)
+        fetch_by_group(1)
+        fetch_by_all(1, 0, O)
+        fetch_seats(3)
+        short_codes = keep.tile([P, O], U32, name="short_codes", tag="slot_codes", align_bytes=64)
+        short_scales = keep.tile([P, O], U8, name="short_scales", tag="seats0", align_bytes=64)
         gather_packed(short_codes, x_words, list7, 0, O)
         gather_packed(short_scales, x_scale_rows, list7, 0, O)
+        hid_grouped = keep.tile([P, O, PACK], BF16, name="hid_grouped", tag="slot_scales", align_bytes=64)
+        larger(0, slice(0, O))
+        larger(1, slice(0, O))
+        fetch_by_group(2)
+        fetch_by_all(2, 0, O)
+        larger(2, slice(0, O))
+        fetch_by_group(3)
+
         width = O // 2
         pieces = [(half, h) for half in range(2) for h in range(N // P)]
         sums = {}
@@ -232,9 +262,7 @@ def tile_picked_tokens_largercode_one_chain_further_plain_kernel(
         for half in range(2):
             cols = slice(half * width, (half + 1) * width)
             fetch_by_all(LAST, half * width, width)
-            nc.vector.tensor_tensor(
-                out=hid_grouped[:, cols, LAST], in0=by_group[LAST][:, cols], in1=by_all[LAST][:, cols], op=MAX
-            )
+            larger(LAST, cols)
         for half in range(2):
             quantize(hid_codes, hid_scales, hid_grouped, half * width, width)
 

from contextlib import ExitStack

import concourse.mybir as mybir

K, J, R, T, F, O, S, N = 512, 1024, 512, 2048, 1024, 256, 512, 256
FLOPS = 2 * K * R * J + 2 * R * N * O + 2 * K * N * O

F32 = mybir.dt.float32
BF16 = mybir.dt.bfloat16
I32 = mybir.dt.int32
U32 = mybir.dt.uint32
U16 = mybir.dt.uint16
U8 = mybir.dt.uint8
FP8X4 = mybir.dt.float8_e4m3fn_x4
FP4X4 = mybir.dt.float4_e2m1fn_x4
COPY = mybir.ActivationFunctionType.Copy
MAX = mybir.AluOpType.max

P = 128
PACK = 4
LAST = PACK - 1
LANES = 16
BANK = 512
QUADRANTS = 4


def tile_picked_tokens_largercode_one_chain_further_plain_kernel(
    tc, xt_words, xt_scales, ua, ub, ha, hb, sa, sb, sd, wb_words, wb_scales, ws_words, ws_scales,
    offs, offs2, offs3, offs4, offs5, offs6, offs7, out,
):
    nc = tc.nc
    with ExitStack() as ctx:
        lists = ctx.enter_context(tc.tile_pool(name="lists", bufs=1))
        keep = ctx.enter_context(tc.tile_pool(name="keep", bufs=1))
        psum = ctx.enter_context(tc.psum_pool(name="psum", bufs=1))

        def load_list(name, source):
            tile = lists.tile(list(source.shape), U16, name=name)
            nc.sync.dma_start(tile[:], source)
            return tile

        def load_factors(name, source, queue):
            tile = keep.tile([P, PACK], F32, name=name)
            queue.dma_start(tile[:], source.rearrange("(p t) o -> p (t o)", t=PACK))
            return tile

        def load_rows(name, source, t):
            tile = keep.tile([P, F], F32, name=name)
            nc.sync.dma_start(tile[:], source.rearrange("(p t) f -> p t f", t=PACK)[:, t, :])
            return tile

        def cleared_plane(name, width):
            tile = keep.tile([P, width], U8, name=name, align_bytes=64)
            nc.vector.memset(tile[:].bitcast(I32), 0)
            return tile

        def load_scale_rows(tile, source, q):
            nc.sync.dma_start(
                tile[32 * q : 32 * q + 4, :].bitcast(I32),
                source[0, 4 * q : 4 * q + 4, :].bitcast(I32),
            )

        def load_fp4_words(name, source):
            tile = keep.tile([P, 2 * N], U8, name=name, align_bytes=64)
            nc.sync.dma_start(tile[:].bitcast(I32), source[0].bitcast(I32))
            return tile

        def fetch(dst, window, offsets, first, count, factor):
            cols = slice(first // LANES, (first + count) // LANES)
            nc.scalar.activation(
                out=dst[:, first : first + count],
                in_=window[:].indirect(offsets[:, cols]),
                func=COPY,
                scale=factor,
            )

        def gather_packed(dst, window, offsets, first, count):
            cols = slice(first // LANES, (first + count) // LANES)
            nc.vector.tensor_copy(out=dst[:, first : first + count], in_=window[:].indirect(offsets[:, cols]))

        def quantize(codes, scales, grouped, first, count):
            nc.vector.quantize_mx(
                out=codes[:, first : first + count].bitcast(FP8X4),
                scales=scales[:, first : first + count],
                in_=grouped[:, first : first + count, :].rearrange("p c t -> p (c t)"),
            )

        x_scale_rows = cleared_plane("x_scale_rows", T)
        ws_scale_rows = cleared_plane("ws_scale_rows", N)
        wb_scale_rows = cleared_plane("wb_scale_rows", N)
        ha_t = load_factors("ha_t", ha, nc.scalar)
        hb_t = load_factors("hb_t", hb, nc.scalar)
        ua_rows, ub_rows = [], []
        list2 = load_list("list2", offs2)
        ua_rows.append(load_rows("ua0", ua, 0))
        list3 = load_list("list3", offs3)
        x_scale_staged = keep.tile([P, 2, T], U8, name="x_scale_staged")
        for half in range(2):
            nc.sync.dma_start(
                x_scale_staged[64 * half : 64 * half + 4, :, :].bitcast(I32),
                xt_scales[0, 8 * half : 8 * half + 8, :].rearrange("(q r) c -> r q c", q=2).bitcast(I32),
            )
        for q in range(QUADRANTS):
            source = 64 * (q // 2)
            nc.vector.tensor_copy(
                out=x_scale_rows[32 * q : 32 * q + 4, :].bitcast(I32),
                in_=x_scale_staged[source : source + 4, q % 2, :].bitcast(I32),
            )
        ub_rows.append(load_rows("ub0", ub, 0))
        list1 = load_list("list1", offs)
        ua_rows.append(load_rows("ua1", ua, 1))
        ub_rows.append(load_rows("ub1", ub, 1))
        ua_rows.append(load_rows("ua2", ua, 2))
        x_words = keep.tile([P, T], U32, name="x_words")
        nc.sync.dma_start(x_words[:].bitcast(I32), xt_words[0].rearrange("p c t -> p (c t)").bitcast(I32))
        ub_rows.append(load_rows("ub2", ub, 2))
        ua_rows.append(load_rows("ua3", ua, 3))
        ub_rows.append(load_rows("ub3", ub, 3))
        list4 = load_list("list4", offs4)
        sa_t = load_factors("sa_t", sa, nc.sync)
        list5 = load_list("list5", offs5)
        sb_t = load_factors("sb_t", sb, nc.sync)
        list6 = load_list("list6", offs6)
        sd_t = load_factors("sd_t", sd, nc.sync)
        list7 = load_list("list7", offs7)
        ws_codes = load_fp4_words("ws_codes", ws_words)
        wb_codes = load_fp4_words("wb_codes", wb_words)
        for q in range(QUADRANTS):
            load_scale_rows(ws_scale_rows, ws_scales, q)
        for q in range(QUADRANTS):
            load_scale_rows(wb_scale_rows, wb_scales, q)

        slot_codes = keep.tile([P, J], U32, name="slot_codes", tag="slot_codes", align_bytes=64)
        slot_scales = keep.tile([P, J], U8, name="slot_scales", tag="slot_scales", align_bytes=64)
        first_prod = [keep.tile([P, R], F32, name="first_prod%d" % t) for t in range(PACK)]
        second_prod = [keep.tile([P, R], F32, name="second_prod%d" % t) for t in range(LAST)]
        second_last = [keep.tile([P, R // 2], F32, name="second_last%d" % half) for half in range(2)]
        wc_plain = keep.tile([P, PACK, R], BF16, name="wc_plain")
        wc_first = keep.tile([P, P, PACK], BF16, name="wc_first", align_bytes=64)

        gather_packed(slot_scales, x_scale_rows, list1, 0, J)
        for t in range(LAST):
            fetch(first_prod[t], ua_rows[t], list2, 0, R, ha_t[:, t : t + 1])
            fetch(second_prod[t], ub_rows[t], list3, 0, R, hb_t[:, t : t + 1])
            if t == LAST - 1:
                for first in range(0, J, BANK):
                    gather_packed(slot_codes, x_words, list1, first, BANK)
            nc.vector.tensor_tensor(out=wc_plain[:, t, :], in0=first_prod[t][:], in1=second_prod[t][:], op=MAX)

        dealt = wc_plain[:].rearrange("p t (m u) -> p u m t", u=PACK)
        nc.vector.tensor_copy(out=wc_first[:, :, 0:LAST], in_=dealt[:, 0, :, 0:LAST])
        fetch(first_prod[LAST], ua_rows[LAST], list2, 0, R, ha_t[:, LAST:PACK])
        for half in range(2):
            entries = slice(half * R // 2, (half + 1) * R // 2)
            nc.scalar.activation(
                out=second_last[half][:],
                in_=ub_rows[LAST][:].indirect(list3[:, entries.start // LANES : entries.stop // LANES]),
                func=COPY,
                scale=hb_t[:, LAST:PACK],
            )
            left = first_prod[LAST][:, entries].rearrange("p (m u) -> p m u", u=PACK)
            right = second_last[half][:].rearrange("p (m u) -> p m u", u=PACK)
            nc.vector.tensor_tensor(
                out=wc_first[:, half * P // 2 : (half + 1) * P // 2, LAST], in0=left[:, :, 0], in1=right[:, :, 0], op=MAX
            )
            nc.vector.tensor_tensor(
                out=wc_plain[:, LAST, entries].rearrange("p (m u) -> p m u", u=PACK)[:, :, 1:PACK],
                in0=left[:, :, 1:PACK],
                in1=right[:, :, 1:PACK],
                op=MAX,
            )

        a_rows = [keep.tile([P, J], F32, name="a_rows%d" % u) for u in range(PACK)]
        seats = [keep.tile([P, S], F32, name="seats%d" % u, tag="seats%d" % u, align_bytes=64) for u in range(PACK)]
        by_group, by_all = [], []
        hid_codes = keep.tile([P, O], U32, name="hid_codes", align_bytes=64)
        hid_scales = keep.tile([P, O], U8, name="hid_scales", align_bytes=64)

        def first_product(u, widths, banks):
            if u == 0:
                grouped = wc_first
            else:
                grouped = keep.tile([P, P, PACK], BF16, name="grouped%d" % u, align_bytes=64)
                nc.vector.tensor_copy(out=grouped[:], in_=dealt[:, u, :, :])
            wc_codes = keep.tile([P, P], U32, name="wc_codes%d" % u, tag="wc_codes%d" % u, align_bytes=64)
            wc_scales = keep.tile([P, P], U8, name="wc_scales%d" % u, tag="wc_scales%d" % u, align_bytes=64)
            quantize(wc_codes, wc_scales, grouped, 0, P)
            first = 0
            for width, bank in zip(widths, banks):
                cols = slice(first, first + width)
                acc = psum.tile([P, width], F32, name="acc", tag="bank%d" % bank)
                nc.tensor.matmul_mx(
                    out=acc[:],
                    lhsT=wc_codes[:].bitcast(FP8X4),
                    lhsT_scale=wc_scales[:],
                    rhs=slot_codes[:, cols].bitcast(FP8X4),
                    rhs_scale=slot_scales[:, cols],
                    start=True,
                    stop=True,
                )
                if u == 0:
                    nc.scalar.copy(out=a_rows[u][:, cols], in_=acc[:])
                else:
                    nc.vector.tensor_copy(out=a_rows[u][:, cols], in_=acc[:])
                first += width

        def fetch_seats(u):
            fetch(seats[u], a_rows[u], list4, 0, S, sa_t[:, u : u + 1])

        def fetch_by_group(u):
            by_group.append(keep.tile([P, O], F32, name="by_group", tag="wc_codes%d" % (2 + u % 2), align_bytes=64))
            by_all.append(keep.tile([P, O], F32, name="by_all", tag="wc_scales%d" % (2 + u % 2), align_bytes=64))
            fetch(by_group[u], seats[u], list5, 0, O, sb_t[:, u : u + 1])

        def fetch_by_all(u, first, count):
            fetch(by_all[u], seats[u], list6, first, count, sd_t[:, u : u + 1])

        first_product(0, [256, 256, 256, 256], [0, 1, 2, 3])
        fetch_seats(0)
        first_product(1, [256, 256, 256, 256], [4, 5, 6, 7])
        fetch_seats(1)
        first_product(2, [BANK, BANK], [0, 7])
        first_product(3, [BANK, BANK], [1, 7])

        def larger(u, cols):
            nc.vector.tensor_tensor(out=hid_grouped[:, cols, u], in0=by_group[u][:, cols], in1=by_all[u][:, cols], op=MAX)

        fetch_by_group(0)
        fetch_by_all(0, 0, O)
        fetch_seats(2)
        fetch_by_group(1)
        fetch_by_all(1, 0, O)
        fetch_seats(3)
        short_codes = keep.tile([P, O], U32, name="short_codes", tag="slot_codes", align_bytes=64)
        short_scales = keep.tile([P, O], U8, name="short_scales", tag="seats0", align_bytes=64)
        gather_packed(short_codes, x_words, list7, 0, O)
        gather_packed(short_scales, x_scale_rows, list7, 0, O)
        hid_grouped = keep.tile([P, O, PACK], BF16, name="hid_grouped", tag="slot_scales", align_bytes=64)
        larger(0, slice(0, O))
        larger(1, slice(0, O))
        fetch_by_group(2)
        fetch_by_all(2, 0, O)
        larger(2, slice(0, O))
        fetch_by_group(3)

        width = O // 2
        pieces = [(half, h) for half in range(2) for h in range(N // P)]
        sums = {}
        for i, (half, h) in enumerate(pieces):
            sums[half, h] = psum.tile([P, width], F32, name="sums", tag="bank%d" % (2 + i))
            cols = slice(half * width, (half + 1) * width)
            nc.tensor.matmul_mx(
                out=sums[half, h][:],
                lhsT=ws_codes[:, 2 * P * h : 2 * P * (h + 1)].bitcast(FP4X4),
                lhsT_scale=ws_scale_rows[:, P * h : P * (h + 1)],
                rhs=short_codes[:, cols].bitcast(FP8X4),
                rhs_scale=short_scales[:, cols],
                start=True,
                stop=False,
            )

        for half in range(2):
            cols = slice(half * width, (half + 1) * width)
            fetch_by_all(LAST, half * width, width)
            larger(LAST, cols)
        for half in range(2):
            quantize(hid_codes, hid_scales, hid_grouped, half * width, width)

        for half, h in pieces:
            cols = slice(half * width, (half + 1) * width)
            nc.tensor.matmul_mx(
                out=sums[half, h][:],
                lhsT=wb_codes[:, 2 * P * h : 2 * P * (h + 1)].bitcast(FP4X4),
                lhsT_scale=wb_scale_rows[:, P * h : P * (h + 1)],
                rhs=hid_codes[:, cols].bitcast(FP8X4),
                rhs_scale=hid_scales[:, cols],
                start=False,
                stop=True,
            )
            result = keep.tile([P, width], F32, name="result%d%d" % (half, h))
            if h == 0:
                nc.vector.tensor_copy(out=result[:], in_=sums[half, h][:])
                nc.sync.dma_start(out[P * h : P * (h + 1), cols], result[:])
            else:
                nc.scalar.copy(out=result[:], in_=sums[half, h][:])
                nc.scalar.dma_start(out[P * h : P * (h + 1), cols], result[:])
